import numpy as np, ml_dtypes
CORES = [0,1,2,3,4,5,6,7]
N = 8
def setup_inputs(rng):
    return {"x": rng.standard_normal((N, 128, 256), dtype=np.float32).astype(ml_dtypes.bfloat16)}
def reference(x):
    b = 256 // N
    blocks = x.reshape(N, 128, N, b)
    return {"y": np.ascontiguousarray(blocks.transpose(2, 1, 0, 3)).reshape(N, 128, 256)}

from concourse.bass import DstId, RemoteDMATransfer

SCRATCH = {
    "src": ("sbuf", [128, 256], "bfloat16"),
    "land": ("sbuf", [128, 256], "bfloat16"),
}
SEMAPHORES = ["loaded", "own", "sent", "arrived", "stored"]

ENGINES_PER_SEND = 2


def rank_program(g, core, T, topo):
    rank = T.rank_of(core)
    if rank is None:
        return
    n = len(T.cores)
    b = T.x.shape[1] // n

    def blk(j):
        return slice(j * b, (j + 1) * b)

    g.sync.dma_start(T.src[:], T.x[:]).then_inc(T.sem.loaded, 16)
    g.scalar.dma_start(T.land[:, blk(rank)], T.x[:, blk(rank)]).then_inc(T.sem.own, 16)

    g.wait_ge(T.sem.loaded, 16)
    transfers = []
    for k, j in enumerate([(rank + d) % n for d in range(1, n)]):
        rid, pid, _se = topo.addr(T.cores[j])
        transfers.append(RemoteDMATransfer(
            dst_ids=[DstId(rid=rid, pnc=pid)],
            dma_engine_mask=0b11 << (ENGINES_PER_SEND * k),
            remote_sem=T.sem.arrived,
            src=T.src[:, blk(j)],
            dst=T.land[:, blk(rank)],
        ))
    g.remote_dma_fused(transfers, local_sem=T.sem.sent)

    g.wait_ge(T.sem.arrived, ENGINES_PER_SEND * (n - 1))
    g.wait_ge(T.sem.own, 16)
    g.dma_start(T.y[:], T.land[:]).then_inc(T.sem.stored, 16)
    g.wait_ge(T.sem.sent, ENGINES_PER_SEND * (n - 1))
    g.wait_ge(T.sem.stored, 16)
